import numpy as np
import ml_dtypes


def mxq(x, axis, fmt="e4m3"):
    dtype, down = {"e4m3": (ml_dtypes.float8_e4m3fn, 7), "e5m2": (ml_dtypes.float8_e5m2, 14)}[fmt]
    v = np.moveaxis(np.asarray(x, np.float32).astype(ml_dtypes.bfloat16).astype(np.float64), axis, -1)
    blocks = v.reshape(v.shape[:-1] + (-1, 32))
    amax = np.abs(blocks).max(-1, keepdims=True)
    byte = np.maximum(np.where(amax > 0, np.frexp(amax)[1] - 1 + 127, 0) - down, 1)
    scale = np.exp2(byte - 127.0)
    codes = (blocks / scale).astype(np.float32).astype(dtype).astype(np.float64)
    return np.moveaxis((codes * scale).reshape(v.shape), -1, axis)


WIDE = False


def mx_kscale(k):
    if not WIDE:
        return np.ones(k)
    levels = np.array([10, -10, 5, -5, 0])
    if k % 512:
        return np.exp2(np.random.permutation(np.resize(levels, k // 32))).repeat(32)
    a = np.empty((k // 512, 16))
    for p in range(k // 512):
        a[p, :8] = np.random.permutation(np.resize(levels, 8))
        for g in range(8):
            far = levels[np.abs(levels - a[p, g]) >= 10]
            a[p, g + 8] = far[np.random.randint(len(far))]
    return np.exp2(a.ravel()).repeat(32)


def f64(x):
    return np.asarray(x).astype(np.float64)


def striped(idx):
    return np.tile(np.asarray(idx).reshape(-1, 16).T, (8, 1)).astype(np.uint16)


def unstriped(offs):
    return offs[:16].T.reshape(-1).astype(np.int64)


E2M1 = np.array([0.0, 0.5, 1.0, 1.5, 2.0, 3.0, 4.0, 6.0, -0.0, -0.5, -1.0, -1.5, -2.0, -3.0, -4.0, -6.0])


def pack_weight(w, fmt):
    k, n = w.shape
    w = f64(np.asarray(w, np.float32).astype(ml_dtypes.bfloat16)).reshape(k // 32, 32, n)
    amax = np.abs(w).max(1)
    if fmt == "e4m3":
        byte = np.frexp(amax)[1] - 1 + 127 - 7
    else:
        mant, ex = np.frexp(amax / 6.0)
        byte = np.where(mant > 0.5, ex, ex - 1) + 127
    byte = np.clip(np.where(amax > 0, byte, 1), 1, 254)
    scaled = (w * np.exp2(127.0 - byte)[:, None, :]).reshape(k, n).astype(np.float32)
    by_word = np.ascontiguousarray(scaled.reshape(k // 512, 128, 4, n).transpose(0, 1, 3, 2))
    if fmt == "e4m3":
        words = by_word.astype(ml_dtypes.float8_e4m3fn).view(np.uint8)
    else:
        c = by_word.astype(ml_dtypes.float4_e2m1fn).view(np.uint8) & 0xF
        words = (c[..., 0::2] | (c[..., 1::2] << 4)).reshape(k // 512, 128, 2 * n)
    return np.ascontiguousarray(words), np.ascontiguousarray(byte.astype(np.uint8).reshape(k // 512, 16, n))


def unpack_weight(words, scales, fmt):
    g, _, n = scales.shape
    words = np.ascontiguousarray(words).reshape(g, 128, n, -1)
    if fmt == "e4m3":
        vals = words.view(ml_dtypes.float8_e4m3fn).astype(np.float64)
    else:
        nib = np.empty((g, 128, n, 4), np.uint8)
        nib[..., 0::2] = words & 0xF
        nib[..., 1::2] = words >> 4
        vals = E2M1[nib]
    vals = vals * np.repeat(np.exp2(scales.astype(np.float64) - 127.0), 8, axis=1)[..., None]
    return vals.transpose(0, 1, 3, 2).reshape(g * 512, n)


def bf(x):
    return np.asarray(x, np.float32).astype(ml_dtypes.bfloat16)


def planes(Y):
    r, m = Y.shape
    b = f64(bf(Y)).reshape(r // 32, 32, m)
    amax = np.abs(b).max(1)
    byte = np.clip(np.where(amax > 0, np.frexp(amax)[1] - 1 + 127 - 7, 1), 1, 254)
    codes = (b * np.exp2(127.0 - byte)[:, None, :]).reshape(r, m).astype(np.float32).astype(ml_dtypes.float8_e4m3fn).view(np.uint8)
    words = codes.reshape(r // 512, 128, 4, m).transpose(0, 1, 3, 2)
    return np.ascontiguousarray(words), np.ascontiguousarray(byte.astype(np.uint8).reshape(r // 512, 16, m))


K, C, L, T, N = 512, 512, 512, 1024, 512


def setup_inputs():
    n = np.random.standard_normal
    idx = np.random.randint(0, C, T)
    fk = mx_kscale(K)
    fl = mx_kscale(L)
    xcp = pack_weight(n((K, C)) / fk[:, None], "e4m3")
    wcp = pack_weight(n((K, N)) * 1 / np.sqrt(K) * fk[:, None], "e2m1")
    xfp = pack_weight(n((L, T)) / fl[:, None], "e2m1")
    return {
        "xc_words": xcp[0],
        "xc_scales": xcp[1],
        "wc_words": wcp[0],
        "wc_scales": wcp[1],
        "xf_words": xfp[0],
        "xf_scales": xfp[1],
        "wf": (n((L, N)) * 1 / np.sqrt(L) * fl[:, None]).astype(np.float32),
        "offs": striped(idx),
    }


def reference(xc_words, xc_scales, wc_words, wc_scales, xf_words, xf_scales, wf, offs):
    idx = unstriped(offs)
    xcu = unpack_weight(xc_words, xc_scales, "e4m3")
    wcu = unpack_weight(wc_words, wc_scales, "e2m1")
    xfu = unpack_weight(xf_words, xf_scales, "e2m1")
    zc = wcu.T @ xcu
    wfq = mxq(f64(wf), 0, "e4m3")
    zf = wfq.T @ xfu
    y = np.maximum(zc[:, idx] + zf, 0.0)
    words, scales = planes(y)
    return y, words, scales

@@ -1,0 +1,198 @@
+from contextlib import ExitStack
+
+import concourse.mybir as mybir
+
+K, C, L, T, N = 512, 512, 512, 1024, 512
+FLOPS = 2 * K * N * C + 2 * L * N * T
+
+F32 = mybir.dt.float32
+BF16 = mybir.dt.bfloat16
+I32 = mybir.dt.int32
+U32 = mybir.dt.uint32
+U16 = mybir.dt.uint16
+U8 = mybir.dt.uint8
+FP8X4 = mybir.dt.float8_e4m3fn_x4
+FP4X4 = mybir.dt.float4_e2m1fn_x4
+ADD = mybir.AluOpType.add
+MAX = mybir.AluOpType.max
+RELU = mybir.ActivationFunctionType.Relu
+
+P = 128
+PACK = 4
+BANK = 512
+WIDTHS = [256, 256, 256, 128, 128]
+STARTS = [sum(WIDTHS[:c]) for c in range(len(WIDTHS))]
+LAST = len(WIDTHS) - 1
+HALF = N // 2
+
+
+def tile_list_coarse_parents_fine_pl_kernel(
+    tc, xc_words, xc_scales, wc_words, wc_scales, xf_words, xf_scales, wf, offs, out_0, out_1, out_2
+):
+    nc = tc.nc
+    with ExitStack() as ctx:
+        keep = ctx.enter_context(tc.tile_pool(name="keep", bufs=1))
+        psum_c = ctx.enter_context(tc.psum_pool(name="psum_c", bufs=1))
+        psum_f = ctx.enter_context(tc.psum_pool(name="psum_f", bufs=4))
+
+        def load_scales(plane, rows):
+            for q in range(4):
+                nc.sync.dma_start(
+                    out=plane[32 * q : 32 * q + 4, :].bitcast(I32), in_=rows[0, 4 * q : 4 * q + 4, :].bitcast(I32)
+                )
+
+        offsets = keep.tile([P, T // 16], U16, name="offsets")
+        wc_raw = keep.tile([P, 2 * N], U8, name="wc_raw", align_bytes=64)
+        wc_raw_scale = keep.tile([P, N], U8, name="wc_raw_scale", align_bytes=64)
+        xc_code = keep.tile([P, C], U32, name="xc_code", align_bytes=64)
+        xc_scale = keep.tile([P, C], U8, name="xc_scale", align_bytes=64)
+        xf_code = keep.tile([P, 2 * T], U8, name="xf_code", align_bytes=64)
+        xf_scale = keep.tile([P, T], U8, name="xf_scale", align_bytes=64)
+        wf_raw = [keep.tile([P, PACK, HALF], F32, name=f"wf_raw{a}", align_bytes=64) for a in range(2)]
+
+        nc.gpsimd.memset(wc_raw_scale[:].bitcast(I32), 0)
+
+        wf_rows = wf.rearrange("(p i) n -> p i n", i=PACK)
+        nc.sync.dma_start(out=wc_raw[:].bitcast(I32), in_=wc_words[0].bitcast(I32))
+        nc.sync.dma_start(
+            out=xc_code[:].bitcast(I32), in_=xc_words[0].rearrange("p c r -> p (c r)").bitcast(I32)
+        )
+        load_scales(wc_raw_scale, wc_scales)
+        load_scales(xc_scale, xc_scales)
+        nc.sync.dma_start(out=wf_raw[0][:], in_=wf_rows[:, :, :HALF])
+        nc.sync.dma_start(out=wf_raw[1][:], in_=wf_rows[:, :, HALF:])
+        nc.sync.dma_start(out=xf_code[:].bitcast(I32), in_=xf_words[0].bitcast(I32))
+        load_scales(xf_scale, xf_scales)
+        nc.sync.dma_start(offsets[:], offs)
+
+        wc_code = keep.tile([P, PACK, 2 * P], U8, name="wc_code", align_bytes=64)
+        wc_scale = keep.tile([P, PACK, P], U8, name="wc_scale", align_bytes=64)
+        nc.vector.tensor_copy(
+            out=wc_code[:].bitcast(U16).rearrange("p j m -> p m j"),
+            in_=wc_raw[:].bitcast(U16).rearrange("p (m j) -> p m j", j=PACK),
+        )
+        nc.vector.tensor_copy(
+            out=wc_scale[:].rearrange("p j m -> p m j"),
+            in_=wc_raw_scale[:].rearrange("p (m j) -> p m j", j=PACK),
+        )
+
+        zc = []
+        for j in range(PACK):
+            bank = psum_c.tile([P, C], F32, name=f"zc_bank{j}")
+            nc.tensor.matmul_mx(
+                out=bank[:],
+                lhsT=wc_code[:, j, :].bitcast(FP4X4),
+                lhsT_scale=wc_scale[:, j, :],
+                rhs=xc_code[:].bitcast(FP8X4),
+                rhs_scale=xc_scale[:],
+                start=True,
+                stop=True,
+            )
+            window = keep.tile([P, C], F32, name=f"zc{j}", align_bytes=64)
+            nc.scalar.copy(out=window[:], in_=bank[:])
+            zc.append(window)
+
+        wf_grouped = keep.tile([P, PACK, P, PACK], BF16, name="wf_grouped", align_bytes=64)
+        wf_code = keep.tile([P, N], U32, name="wf_code", align_bytes=64)
+        wf_scale = keep.tile([P, N], U8, name="wf_scale", align_bytes=64)
+        wf_dst = wf_grouped[:].rearrange("p j m i -> p m i j")
+        for a in range(2):
+            nc.vector.tensor_copy(
+                out=wf_dst[:, a * P // 2 : (a + 1) * P // 2],
+                in_=wf_raw[a][:].rearrange("p i (m j) -> p m i j", j=PACK),
+            )
+        for h in range(2):
+            nc.vector.quantize_mx(
+                out=wf_code[:, h * HALF : (h + 1) * HALF].bitcast(FP8X4),
+                scales=wf_scale[:, h * HALF : (h + 1) * HALF],
+                in_=wf_grouped[:, 2 * h : 2 * h + 2].rearrange("p j m i -> p (j m i)"),
+            )
+
+        zf = {}
+        summed = {}
+        rounded = {}
+        y_code = keep.tile([P, T], U32, name="y_code", align_bytes=64)
+        y_scale = keep.tile([P, T], U8, name="y_scale", align_bytes=64)
+
+        def fine(c):
+            t0, width = STARTS[c], WIDTHS[c]
+            per_bank = BANK // width
+            for j0 in range(0, PACK, per_bank):
+                bank = psum_f.tile([P, per_bank, width], F32, name="zf_bank")
+                for u in range(per_bank):
+                    cols = slice((j0 + u) * P, (j0 + u + 1) * P)
+                    nc.tensor.matmul_mx(
+                        out=bank[:, u, :],
+                        lhsT=wf_code[:, cols].bitcast(FP8X4),
+                        lhsT_scale=wf_scale[:, cols],
+                        rhs=xf_code[:, 2 * t0 : 2 * (t0 + width)].bitcast(FP4X4),
+                        rhs_scale=xf_scale[:, t0 : t0 + width],
+                        start=True,
+                        stop=True,
+                    )
+                rows = keep.tile([P, per_bank, width], F32, name=f"zf{c}_{j0}", tag=f"zf{c}_{j0}", align_bytes=64)
+                nc.scalar.copy(out=rows[:], in_=bank[:])
+                for u in range(per_bank):
+                    zf[c, j0 + u] = rows[:, u, :]
+
+        def gather_add(c):
+            t0, width = STARTS[c], WIDTHS[c]
+            summed[c] = keep.tile([P, PACK, width], F32, name=f"summed{c}", align_bytes=64)
+            listed = offsets[:, t0 // 16 : (t0 + width) // 16]
+            for j in range(PACK):
+                nc.vector.tensor_tensor(out=summed[c][:, j, :], in0=zc[j][:].indirect(listed), in1=zf[c, j], op=ADD)
+
+        def relu(on_vector, dst, src):
+            if on_vector:
+                nc.vector.tensor_scalar(out=dst, in0=src, scalar1=0.0, scalar2=None, op0=MAX)
+            else:
+                nc.scalar.activation(out=dst, in_=src, func=RELU)
+
+        def store_y(c):
+            t0, width = STARTS[c], WIDTHS[c]
+            y = keep.tile([P, PACK, width], F32, name=f"y{c}", align_bytes=64)
+            relu(c == LAST, y[:], summed[c][:])
+            nc.sync.dma_start(out=out_0.rearrange("(p j) t -> p j t", j=PACK)[:, :, t0 : t0 + width], in_=y[:])
+
+        def weave(c):
+            tag = f"zf{LAST}_0" if c == LAST - 1 else f"rounded{c}"
+            rounded[c] = keep.tile([P, WIDTHS[c], PACK], BF16, name=f"rounded{c}", tag=tag, align_bytes=64)
+            relu(
+                c >= LAST - 1,
+                rounded[c][:].rearrange("p (a e) j -> p a j e", e=4),
+                summed[c][:].rearrange("p j (a e) -> p a j e", e=4),
+            )
+
+        def quantise(c):
+            cols = slice(STARTS[c], STARTS[c] + WIDTHS[c])
+            nc.vector.quantize_mx(
+                out=y_code[:, cols].bitcast(FP8X4),
+                scales=y_scale[:, cols],
+                in_=rounded[c][:].rearrange("p t j -> p (t j)"),
+            )
+            nc.sync.dma_start(
+                out=out_1[0].rearrange("p t r -> p (t r)").bitcast(I32)[:, cols], in_=y_code[:, cols].bitcast(I32)
+            )
+
+        fine(0)
+        fine(1)
+        for c in range(LAST - 1):
+            fine(c + 2)
+            gather_add(c)
+            store_y(c)
+            weave(c)
+            if c > 0:
+                quantise(c - 1)
+        gather_add(LAST - 1)
+        store_y(LAST - 1)
+        gather_add(LAST)
+        weave(LAST - 1)
+        store_y(LAST)
+        weave(LAST)
+        for c in range(LAST - 2, LAST + 1):
+            quantise(c)
+        for q in range(4):
+            queue = nc.sync if q % 2 == 0 else nc.scalar
+            queue.dma_start(
+                out=out_2[0, 4 * q : 4 * q + 4, :].bitcast(I32), in_=y_scale[32 * q : 32 * q + 4, :].bitcast(I32)
+            )

@@ -23,7 +23,7 @@ BANK = 512
 WIDTHS = [256, 256, 256, 128, 128]
 STARTS = [sum(WIDTHS[:c]) for c in range(len(WIDTHS))]
 LAST = len(WIDTHS) - 1
-HALF = N // 2
+WF_SPLIT = [0, 320, N]
 
 
 def tile_list_coarse_parents_fine_pl_kernel(
@@ -35,9 +35,9 @@ def tile_list_coarse_parents_fine_pl_kernel(
         psum_c = ctx.enter_context(tc.psum_pool(name="psum_c", bufs=1))
         psum_f = ctx.enter_context(tc.psum_pool(name="psum_f", bufs=4))
 
-        def load_scales(plane, rows):
-            for q in range(4):
-                nc.sync.dma_start(
+        def load_scales(queue, plane, rows, quadrants):
+            for q in quadrants:
+                queue.dma_start(
                     out=plane[32 * q : 32 * q + 4, :].bitcast(I32), in_=rows[0, 4 * q : 4 * q + 4, :].bitcast(I32)
                 )
 
@@ -48,21 +48,26 @@ def tile_list_coarse_parents_fine_pl_kernel(
         xc_scale = keep.tile([P, C], U8, name="xc_scale", align_bytes=64)
         xf_code = keep.tile([P, 2 * T], U8, name="xf_code", align_bytes=64)
         xf_scale = keep.tile([P, T], U8, name="xf_scale", align_bytes=64)
-        wf_raw = [keep.tile([P, PACK, HALF], F32, name=f"wf_raw{a}", align_bytes=64) for a in range(2)]
+        wf_raw = [
+            keep.tile([P, PACK, WF_SPLIT[a + 1] - WF_SPLIT[a]], F32, name=f"wf_raw{a}", align_bytes=64)
+            for a in range(len(WF_SPLIT) - 1)
+        ]
 
-        nc.gpsimd.memset(wc_raw_scale[:].bitcast(I32), 0)
+        nc.vector.memset(wc_raw_scale[:].bitcast(I32), 0)
 
         wf_rows = wf.rearrange("(p i) n -> p i n", i=PACK)
         nc.sync.dma_start(out=wc_raw[:].bitcast(I32), in_=wc_words[0].bitcast(I32))
+        load_scales(nc.sync, xc_scale, xc_scales, range(4))
+        nc.sync.dma_start(out=wf_raw[0][:], in_=wf_rows[:, :, : WF_SPLIT[1]])
         nc.sync.dma_start(
             out=xc_code[:].bitcast(I32), in_=xc_words[0].rearrange("p c r -> p (c r)").bitcast(I32)
         )
-        load_scales(wc_raw_scale, wc_scales)
-        load_scales(xc_scale, xc_scales)
-        nc.sync.dma_start(out=wf_raw[0][:], in_=wf_rows[:, :, :HALF])
-        nc.sync.dma_start(out=wf_raw[1][:], in_=wf_rows[:, :, HALF:])
+        load_scales(nc.sync, xf_scale, xf_scales, range(1))
+        load_scales(nc.sync, wc_raw_scale, wc_scales, range(4))
+        for a in range(1, len(wf_raw)):
+            nc.sync.dma_start(out=wf_raw[a][:], in_=wf_rows[:, :, WF_SPLIT[a] : WF_SPLIT[a + 1]])
         nc.sync.dma_start(out=xf_code[:].bitcast(I32), in_=xf_words[0].bitcast(I32))
-        load_scales(xf_scale, xf_scales)
+        load_scales(nc.sync, xf_scale, xf_scales, range(1, 4))
         nc.sync.dma_start(offsets[:], offs)
 
         wc_code = keep.tile([P, PACK, 2 * P], U8, name="wc_code", align_bytes=64)
@@ -76,8 +81,9 @@ def tile_list_coarse_parents_fine_pl_kernel(
             in_=wc_raw_scale[:].rearrange("p (m j) -> p m j", j=PACK),
         )
 
-        zc = []
-        for j in range(PACK):
+        zc = {}
+
+        def coarse(j):
             bank = psum_c.tile([P, C], F32, name=f"zc_bank{j}")
             nc.tensor.matmul_mx(
                 out=bank[:],
@@ -88,24 +94,27 @@ def tile_list_coarse_parents_fine_pl_kernel(
                 start=True,
                 stop=True,
             )
-            window = keep.tile([P, C], F32, name=f"zc{j}", align_bytes=64)
-            nc.scalar.copy(out=window[:], in_=bank[:])
-            zc.append(window)
+            if j == PACK - 1:
+                zc[j] = keep.tile([P, C], F32, name=f"zc{j}", tag="wf_grouped", align_bytes=64)
+                nc.vector.tensor_copy(out=zc[j][:], in_=bank[:])
+            else:
+                zc[j] = keep.tile([P, C], F32, name=f"zc{j}", align_bytes=64)
+                nc.scalar.copy(out=zc[j][:], in_=bank[:])
 
-        wf_grouped = keep.tile([P, PACK, P, PACK], BF16, name="wf_grouped", align_bytes=64)
-        wf_code = keep.tile([P, N], U32, name="wf_code", align_bytes=64)
-        wf_scale = keep.tile([P, N], U8, name="wf_scale", align_bytes=64)
+        wf_grouped = keep.tile([P, PACK, P, PACK], BF16, name="wf_grouped", tag="wf_grouped", align_bytes=64)
+        wf_code = [keep.tile([P, P], U32, name=f"wf_code{j}", align_bytes=64) for j in range(PACK)]
+        wf_scale = [keep.tile([P, P], U8, name=f"wf_scale{j}", align_bytes=64) for j in range(PACK)]
         wf_dst = wf_grouped[:].rearrange("p j m i -> p m i j")
-        for a in range(2):
-            nc.vector.tensor_copy(
-                out=wf_dst[:, a * P // 2 : (a + 1) * P // 2],
+        for a, copy in enumerate((nc.scalar.copy, nc.vector.tensor_copy)):
+            copy(
+                out=wf_dst[:, WF_SPLIT[a] // PACK : WF_SPLIT[a + 1] // PACK],
                 in_=wf_raw[a][:].rearrange("p i (m j) -> p m i j", j=PACK),
             )
-        for h in range(2):
+        for j in range(PACK):
             nc.vector.quantize_mx(
-                out=wf_code[:, h * HALF : (h + 1) * HALF].bitcast(FP8X4),
-                scales=wf_scale[:, h * HALF : (h + 1) * HALF],
-                in_=wf_grouped[:, 2 * h : 2 * h + 2].rearrange("p j m i -> p (j m i)"),
+                out=wf_code[j][:].bitcast(FP8X4),
+                scales=wf_scale[j][:],
+                in_=wf_grouped[:, j].rearrange("p m i -> p (m i)"),
             )
 
         zf = {}
@@ -114,17 +123,16 @@ def tile_list_coarse_parents_fine_pl_kernel(
         y_code = keep.tile([P, T], U32, name="y_code", align_bytes=64)
         y_scale = keep.tile([P, T], U8, name="y_scale", align_bytes=64)
 
-        def fine(c):
+        def fine(c, slices=range(PACK)):
             t0, width = STARTS[c], WIDTHS[c]
-            per_bank = BANK // width
-            for j0 in range(0, PACK, per_bank):
+            per_bank = 1 if c == 0 else BANK // width
+            for j0 in slices[::per_bank]:
                 bank = psum_f.tile([P, per_bank, width], F32, name="zf_bank")
                 for u in range(per_bank):
-                    cols = slice((j0 + u) * P, (j0 + u + 1) * P)
                     nc.tensor.matmul_mx(
                         out=bank[:, u, :],
-                        lhsT=wf_code[:, cols].bitcast(FP8X4),
-                        lhsT_scale=wf_scale[:, cols],
+                        lhsT=wf_code[j0 + u][:].bitcast(FP8X4),
+                        lhsT_scale=wf_scale[j0 + u][:],
                         rhs=xf_code[:, 2 * t0 : 2 * (t0 + width)].bitcast(FP4X4),
                         rhs_scale=xf_scale[:, t0 : t0 + width],
                         start=True,
@@ -151,7 +159,7 @@ def tile_list_coarse_parents_fine_pl_kernel(
         def store_y(c):
             t0, width = STARTS[c], WIDTHS[c]
             y = keep.tile([P, PACK, width], F32, name=f"y{c}", align_bytes=64)
-            relu(c == LAST, y[:], summed[c][:])
+            relu(False, y[:], summed[c][:])
             nc.sync.dma_start(out=out_0.rearrange("(p j) t -> p j t", j=PACK)[:, :, t0 : t0 + width], in_=y[:])
 
         def weave(c):
@@ -174,6 +182,8 @@ def tile_list_coarse_parents_fine_pl_kernel(
                 out=out_1[0].rearrange("p t r -> p (t r)").bitcast(I32)[:, cols], in_=y_code[:, cols].bitcast(I32)
             )
 
+        for j in range(PACK):
+            coarse(j)
         fine(0)
         fine(1)
         for c in range(LAST - 1):

@@ -73,18 +73,18 @@ def tile_list_coarse_parents_fine_pl_kernel(
         wc_code = keep.tile([P, PACK, 2 * P], U8, name="wc_code", align_bytes=64)
         wc_scale = keep.tile([P, PACK, P], U8, name="wc_scale", align_bytes=64)
         nc.vector.tensor_copy(
-            out=wc_code[:].bitcast(U16).rearrange("p j m -> p m j"),
-            in_=wc_raw[:].bitcast(U16).rearrange("p (m j) -> p m j", j=PACK),
+            out=wc_code[:].bitcast(U16),
+            in_=wc_raw[:].bitcast(U16).rearrange("p (m j) -> p j m", j=PACK),
         )
         nc.vector.tensor_copy(
-            out=wc_scale[:].rearrange("p j m -> p m j"),
-            in_=wc_raw_scale[:].rearrange("p (m j) -> p m j", j=PACK),
+            out=wc_scale[:],
+            in_=wc_raw_scale[:].rearrange("p (m j) -> p j m", j=PACK),
         )
 
         zc = {}
 
         def coarse(j):
-            bank = psum_c.tile([P, C], F32, name=f"zc_bank{j}")
+            bank = psum_c.tile([P, C], F32, name=f"zc_bank{j}", tag=f"coarse{j}")
             nc.tensor.matmul_mx(
                 out=bank[:],
                 lhsT=wc_code[:, j, :].bitcast(FP4X4),
@@ -94,7 +94,7 @@ def tile_list_coarse_parents_fine_pl_kernel(
                 start=True,
                 stop=True,
             )
-            if j == PACK - 1:
+            if j == PACK - 2:
                 zc[j] = keep.tile([P, C], F32, name=f"zc{j}", tag="wf_grouped", align_bytes=64)
                 nc.vector.tensor_copy(out=zc[j][:], in_=bank[:])
             else:
@@ -104,11 +104,11 @@ def tile_list_coarse_parents_fine_pl_kernel(
         wf_grouped = keep.tile([P, PACK, P, PACK], BF16, name="wf_grouped", tag="wf_grouped", align_bytes=64)
         wf_code = [keep.tile([P, P], U32, name=f"wf_code{j}", align_bytes=64) for j in range(PACK)]
         wf_scale = [keep.tile([P, P], U8, name=f"wf_scale{j}", align_bytes=64) for j in range(PACK)]
-        wf_dst = wf_grouped[:].rearrange("p j m i -> p m i j")
+        wf_dst = wf_grouped[:].rearrange("p j m i -> p m j i")
         for a, copy in enumerate((nc.scalar.copy, nc.vector.tensor_copy)):
             copy(
                 out=wf_dst[:, WF_SPLIT[a] // PACK : WF_SPLIT[a + 1] // PACK],
-                in_=wf_raw[a][:].rearrange("p i (m j) -> p m i j", j=PACK),
+                in_=wf_raw[a][:].rearrange("p i (m j) -> p m j i", j=PACK),
             )
         for j in range(PACK):
             nc.vector.quantize_mx(
@@ -127,7 +127,10 @@ def tile_list_coarse_parents_fine_pl_kernel(
             t0, width = STARTS[c], WIDTHS[c]
             per_bank = 1 if c == 0 else BANK // width
             for j0 in slices[::per_bank]:
-                bank = psum_f.tile([P, per_bank, width], F32, name="zf_bank")
+                if (c, j0) == (0, 0):
+                    bank = psum_c.tile([P, per_bank, width], F32, name="zf_first", tag=f"coarse{PACK - 1}")
+                else:
+                    bank = psum_f.tile([P, per_bank, width], F32, name="zf_bank")
                 for u in range(per_bank):
                     nc.tensor.matmul_mx(
                         out=bank[:, u, :],
@@ -182,9 +185,11 @@ def tile_list_coarse_parents_fine_pl_kernel(
                 out=out_1[0].rearrange("p t r -> p (t r)").bitcast(I32)[:, cols], in_=y_code[:, cols].bitcast(I32)
             )
 
-        for j in range(PACK):
+        for j in range(PACK - 1):
             coarse(j)
-        fine(0)
+        fine(0, range(PACK - 1))
+        coarse(PACK - 1)
+        fine(0, range(PACK - 1, PACK))
         fine(1)
         for c in range(LAST - 1):
             fine(c + 2)

from contextlib import ExitStack

import concourse.mybir as mybir

K, C, L, T, N = 512, 512, 512, 1024, 512
FLOPS = 2 * K * N * C + 2 * L * N * T

F32 = mybir.dt.float32
BF16 = mybir.dt.bfloat16
I32 = mybir.dt.int32
U32 = mybir.dt.uint32
U16 = mybir.dt.uint16
U8 = mybir.dt.uint8
FP8X4 = mybir.dt.float8_e4m3fn_x4
FP4X4 = mybir.dt.float4_e2m1fn_x4
ADD = mybir.AluOpType.add
MAX = mybir.AluOpType.max
RELU = mybir.ActivationFunctionType.Relu

P = 128
PACK = 4
BANK = 512
WIDTHS = [256, 256, 256, 128, 128]
STARTS = [sum(WIDTHS[:c]) for c in range(len(WIDTHS))]
LAST = len(WIDTHS) - 1
WF_SPLIT = [0, 320, N]


def tile_list_coarse_parents_fine_pl_kernel(
    tc, xc_words, xc_scales, wc_words, wc_scales, xf_words, xf_scales, wf, offs, out_0, out_1, out_2
):
    nc = tc.nc
    with ExitStack() as ctx:
        keep = ctx.enter_context(tc.tile_pool(name="keep", bufs=1))
        psum_c = ctx.enter_context(tc.psum_pool(name="psum_c", bufs=1))
        psum_f = ctx.enter_context(tc.psum_pool(name="psum_f", bufs=4))

        def load_scales(queue, plane, rows, quadrants):
            for q in quadrants:
                queue.dma_start(
                    out=plane[32 * q : 32 * q + 4, :].bitcast(I32), in_=rows[0, 4 * q : 4 * q + 4, :].bitcast(I32)
                )

        offsets = keep.tile([P, T // 16], U16, name="offsets")
        wc_raw = keep.tile([P, 2 * N], U8, name="wc_raw", align_bytes=64)
        wc_raw_scale = keep.tile([P, N], U8, name="wc_raw_scale", align_bytes=64)
        xc_code = keep.tile([P, C], U32, name="xc_code", align_bytes=64)
        xc_scale = keep.tile([P, C], U8, name="xc_scale", align_bytes=64)
        xf_code = keep.tile([P, 2 * T], U8, name="xf_code", align_bytes=64)
        xf_scale = keep.tile([P, T], U8, name="xf_scale", align_bytes=64)
        wf_raw = [
            keep.tile([P, PACK, WF_SPLIT[a + 1] - WF_SPLIT[a]], F32, name=f"wf_raw{a}", align_bytes=64)
            for a in range(len(WF_SPLIT) - 1)
        ]

        nc.vector.memset(wc_raw_scale[:].bitcast(I32), 0)

        wf_rows = wf.rearrange("(p i) n -> p i n", i=PACK)
        nc.sync.dma_start(out=wc_raw[:].bitcast(I32), in_=wc_words[0].bitcast(I32))
        load_scales(nc.sync, xc_scale, xc_scales, range(4))
        nc.sync.dma_start(out=wf_raw[0][:], in_=wf_rows[:, :, : WF_SPLIT[1]])
        nc.sync.dma_start(
            out=xc_code[:].bitcast(I32), in_=xc_words[0].rearrange("p c r -> p (c r)").bitcast(I32)
        )
        load_scales(nc.sync, xf_scale, xf_scales, range(1))
        load_scales(nc.sync, wc_raw_scale, wc_scales, range(4))
        for a in range(1, len(wf_raw)):
            nc.sync.dma_start(out=wf_raw[a][:], in_=wf_rows[:, :, WF_SPLIT[a] : WF_SPLIT[a + 1]])
        nc.sync.dma_start(out=xf_code[:].bitcast(I32), in_=xf_words[0].bitcast(I32))
        load_scales(nc.sync, xf_scale, xf_scales, range(1, 4))
        nc.sync.dma_start(offsets[:], offs)

        wc_code = keep.tile([P, PACK, 2 * P], U8, name="wc_code", align_bytes=64)
        wc_scale = keep.tile([P, PACK, P], U8, name="wc_scale", align_bytes=64)
        nc.vector.tensor_copy(
            out=wc_code[:].bitcast(U16),
            in_=wc_raw[:].bitcast(U16).rearrange("p (m j) -> p j m", j=PACK),
        )
        nc.vector.tensor_copy(
            out=wc_scale[:],
            in_=wc_raw_scale[:].rearrange("p (m j) -> p j m", j=PACK),
        )

        zc = {}

        def coarse(j):
            bank = psum_c.tile([P, C], F32, name=f"zc_bank{j}", tag=f"coarse{j}")
            nc.tensor.matmul_mx(
                out=bank[:],
                lhsT=wc_code[:, j, :].bitcast(FP4X4),
                lhsT_scale=wc_scale[:, j, :],
                rhs=xc_code[:].bitcast(FP8X4),
                rhs_scale=xc_scale[:],
                start=True,
                stop=True,
            )
            if j == PACK - 2:
                zc[j] = keep.tile([P, C], F32, name=f"zc{j}", tag="wf_grouped", align_bytes=64)
                nc.vector.tensor_copy(out=zc[j][:], in_=bank[:])
            else:
                zc[j] = keep.tile([P, C], F32, name=f"zc{j}", align_bytes=64)
                nc.scalar.copy(out=zc[j][:], in_=bank[:])

        wf_grouped = keep.tile([P, PACK, P, PACK], BF16, name="wf_grouped", tag="wf_grouped", align_bytes=64)
        wf_code = [keep.tile([P, P], U32, name=f"wf_code{j}", align_bytes=64) for j in range(PACK)]
        wf_scale = [keep.tile([P, P], U8, name=f"wf_scale{j}", align_bytes=64) for j in range(PACK)]
        wf_dst = wf_grouped[:].rearrange("p j m i -> p m j i")
        for a, copy in enumerate((nc.scalar.copy, nc.vector.tensor_copy)):
            copy(
                out=wf_dst[:, WF_SPLIT[a] // PACK : WF_SPLIT[a + 1] // PACK],
                in_=wf_raw[a][:].rearrange("p i (m j) -> p m j i", j=PACK),
            )
        for j in range(PACK):
            nc.vector.quantize_mx(
                out=wf_code[j][:].bitcast(FP8X4),
                scales=wf_scale[j][:],
                in_=wf_grouped[:, j].rearrange("p m i -> p (m i)"),
            )

        zf = {}
        summed = {}
        rounded = {}
        y_code = keep.tile([P, T], U32, name="y_code", align_bytes=64)
        y_scale = keep.tile([P, T], U8, name="y_scale", align_bytes=64)

        def fine(c, slices=range(PACK)):
            t0, width = STARTS[c], WIDTHS[c]
            per_bank = 1 if c == 0 else BANK // width
            for j0 in slices[::per_bank]:
                if (c, j0) == (0, 0):
                    bank = psum_c.tile([P, per_bank, width], F32, name="zf_first", tag=f"coarse{PACK - 1}")
                else:
                    bank = psum_f.tile([P, per_bank, width], F32, name="zf_bank")
                for u in range(per_bank):
                    nc.tensor.matmul_mx(
                        out=bank[:, u, :],
                        lhsT=wf_code[j0 + u][:].bitcast(FP8X4),
                        lhsT_scale=wf_scale[j0 + u][:],
                        rhs=xf_code[:, 2 * t0 : 2 * (t0 + width)].bitcast(FP4X4),
                        rhs_scale=xf_scale[:, t0 : t0 + width],
                        start=True,
                        stop=True,
                    )
                rows = keep.tile([P, per_bank, width], F32, name=f"zf{c}_{j0}", tag=f"zf{c}_{j0}", align_bytes=64)
                nc.scalar.copy(out=rows[:], in_=bank[:])
                for u in range(per_bank):
                    zf[c, j0 + u] = rows[:, u, :]

        def gather_add(c):
            t0, width = STARTS[c], WIDTHS[c]
            summed[c] = keep.tile([P, PACK, width], F32, name=f"summed{c}", align_bytes=64)
            listed = offsets[:, t0 // 16 : (t0 + width) // 16]
            for j in range(PACK):
                nc.vector.tensor_tensor(out=summed[c][:, j, :], in0=zc[j][:].indirect(listed), in1=zf[c, j], op=ADD)

        def relu(on_vector, dst, src):
            if on_vector:
                nc.vector.tensor_scalar(out=dst, in0=src, scalar1=0.0, scalar2=None, op0=MAX)
            else:
                nc.scalar.activation(out=dst, in_=src, func=RELU)

        def store_y(c):
            t0, width = STARTS[c], WIDTHS[c]
            y = keep.tile([P, PACK, width], F32, name=f"y{c}", align_bytes=64)
            relu(False, y[:], summed[c][:])
            nc.sync.dma_start(out=out_0.rearrange("(p j) t -> p j t", j=PACK)[:, :, t0 : t0 + width], in_=y[:])

        def weave(c):
            tag = f"zf{LAST}_0" if c == LAST - 1 else f"rounded{c}"
            rounded[c] = keep.tile([P, WIDTHS[c], PACK], BF16, name=f"rounded{c}", tag=tag, align_bytes=64)
            relu(
                c >= LAST - 1,
                rounded[c][:].rearrange("p (a e) j -> p a j e", e=4),
                summed[c][:].rearrange("p j (a e) -> p a j e", e=4),
            )

        def quantise(c):
            cols = slice(STARTS[c], STARTS[c] + WIDTHS[c])
            nc.vector.quantize_mx(
                out=y_code[:, cols].bitcast(FP8X4),
                scales=y_scale[:, cols],
                in_=rounded[c][:].rearrange("p t j -> p (t j)"),
            )
            nc.sync.dma_start(
                out=out_1[0].rearrange("p t r -> p (t r)").bitcast(I32)[:, cols], in_=y_code[:, cols].bitcast(I32)
            )

        for j in range(PACK - 1):
            coarse(j)
        fine(0, range(PACK - 1))
        coarse(PACK - 1)
        fine(0, range(PACK - 1, PACK))
        fine(1)
        for c in range(LAST - 1):
            fine(c + 2)
            gather_add(c)
            store_y(c)
            weave(c)
            if c > 0:
                quantise(c - 1)
        gather_add(LAST - 1)
        store_y(LAST - 1)
        gather_add(LAST)
        weave(LAST - 1)
        store_y(LAST)
        weave(LAST)
        for c in range(LAST - 2, LAST + 1):
            quantise(c)
        for q in range(4):
            queue = nc.sync if q % 2 == 0 else nc.scalar
            queue.dma_start(
                out=out_2[0, 4 * q : 4 * q + 4, :].bitcast(I32), in_=y_scale[32 * q : 32 * q + 4, :].bitcast(I32)
            )
